import numpy as np
import ml_dtypes


def mxq(x, axis, fmt="e4m3"):
    dtype, down = {"e4m3": (ml_dtypes.float8_e4m3fn, 7), "e5m2": (ml_dtypes.float8_e5m2, 14)}[fmt]
    v = np.moveaxis(np.asarray(x, np.float32).astype(ml_dtypes.bfloat16).astype(np.float64), axis, -1)
    blocks = v.reshape(v.shape[:-1] + (-1, 32))
    amax = np.abs(blocks).max(-1, keepdims=True)
    byte = np.maximum(np.where(amax > 0, np.frexp(amax)[1] - 1 + 127, 0) - down, 1)
    scale = np.exp2(byte - 127.0)
    codes = (blocks / scale).astype(np.float32).astype(dtype).astype(np.float64)
    return np.moveaxis((codes * scale).reshape(v.shape), -1, axis)


WIDE = False


def mx_kscale(k):
    if not WIDE:
        return np.ones(k)
    levels = np.array([10, -10, 5, -5, 0])
    if k % 512:
        return np.exp2(np.random.permutation(np.resize(levels, k // 32))).repeat(32)
    a = np.empty((k // 512, 16))
    for p in range(k // 512):
        a[p, :8] = np.random.permutation(np.resize(levels, 8))
        for g in range(8):
            far = levels[np.abs(levels - a[p, g]) >= 10]
            a[p, g + 8] = far[np.random.randint(len(far))]
    return np.exp2(a.ravel()).repeat(32)


def f64(x):
    return np.asarray(x).astype(np.float64)


def striped(idx):
    return np.tile(idx.reshape(-1, 16).T, (8, 1)).astype(np.uint16)


def unstriped(offs):
    return offs[:16].T.reshape(-1).astype(np.int64)


E2M1 = np.array([0.0, 0.5, 1.0, 1.5, 2.0, 3.0, 4.0, 6.0, -0.0, -0.5, -1.0, -1.5, -2.0, -3.0, -4.0, -6.0])


def pack_weight(w, fmt):
    k, n = w.shape
    w = f64(np.asarray(w, np.float32).astype(ml_dtypes.bfloat16)).reshape(k // 32, 32, n)
    amax = np.abs(w).max(1)
    if fmt == "e4m3":
        byte = np.frexp(amax)[1] - 1 + 127 - 7
    else:
        mant, ex = np.frexp(amax / 6.0)
        byte = np.where(mant > 0.5, ex, ex - 1) + 127
    byte = np.clip(np.where(amax > 0, byte, 1), 1, 254)
    scaled = (w * np.exp2(127.0 - byte)[:, None, :]).reshape(k, n).astype(np.float32)
    by_word = np.ascontiguousarray(scaled.reshape(k // 512, 128, 4, n).transpose(0, 1, 3, 2))
    if fmt == "e4m3":
        words = by_word.astype(ml_dtypes.float8_e4m3fn).view(np.uint8)
    else:
        c = by_word.astype(ml_dtypes.float4_e2m1fn).view(np.uint8) & 0xF
        words = (c[..., 0::2] | (c[..., 1::2] << 4)).reshape(k // 512, 128, 2 * n)
    return np.ascontiguousarray(words), np.ascontiguousarray(byte.astype(np.uint8).reshape(k // 512, 16, n))


def unpack_weight(words, scales, fmt):
    g, _, n = scales.shape
    words = np.ascontiguousarray(words).reshape(g, 128, n, -1)
    if fmt == "e4m3":
        vals = words.view(ml_dtypes.float8_e4m3fn).astype(np.float64)
    else:
        nib = np.empty((g, 128, n, 4), np.uint8)
        nib[..., 0::2] = words & 0xF
        nib[..., 1::2] = words >> 4
        vals = E2M1[nib]
    vals = vals * np.repeat(np.exp2(scales.astype(np.float64) - 127.0), 8, axis=1)[..., None]
    return vals.transpose(0, 1, 3, 2).reshape(g * 512, n)


def gelu(v):
    return 0.5 * v * (1.0 + np.tanh(np.sqrt(2.0 / np.pi) * (v + 0.044715 * v**3)))


K, T, S, S2 = 1024, 2048, 512, 1024

def setup_inputs():
    n = np.random.standard_normal
    s = mx_kscale(K)[:, None]
    c = 0.37 / K**0.5
    perm = np.random.permutation(T)
    d = {}
    d["tab_words"], d["tab_scales"] = pack_weight(n((K, T)) * s, "e4m3")
    d["offs"] = striped(perm[:S])
    d["offs2"] = striped(perm[S:S + S2])
    d["w1_words"], d["w1_scales"] = pack_weight(n((K, K)) * c / K**0.5 / s / s.T, "e2m1")
    d["w2"] = (n((K, K)) * c / K**0.5 / s / s.T).astype(np.float32)
    carry = (0.9 * np.eye(K) + 0.45 * n((K, K)) / K**0.5) * c
    d["w3_words"], d["w3_scales"] = pack_weight(carry / s / s.T, "e4m3")
    d["gain"] = n(K).astype(np.float32)
    d["zest"] = (1.5 * n(S2)).astype(np.float32)
    return d

def reference(tab_words, tab_scales, offs, offs2, w1_words, w1_scales, w2, w3_words, w3_scales, gain, zest):
    TW = unpack_weight(tab_words, tab_scales, "e4m3")
    v = TW[:, unstriped(offs)]
    v2 = TW[:, unstriped(offs2)]
    w1 = unpack_weight(w1_words, w1_scales, "e2m1")
    w3 = unpack_weight(w3_words, w3_scales, "e4m3")
    blend = w1.T @ v
    raw = w3.T @ v
    base = mxq(f64(w2), 0, "e4m3").T @ v
    h = base - np.maximum(blend, f64(gain)[:, None] * raw)
    e = v2.T @ mxq(h, 0, "e4m3")
    return e + f64(zest)[:, None] * np.sin(e)

@@ -1,0 +1,235 @@
+from contextlib import ExitStack
+
+import concourse.mybir as mybir
+
+K, T, S, S2 = 1024, 2048, 512, 1024
+FLOPS = 2 * K * K * S * 3 + 2 * K * S2 * S
+
+F32 = mybir.dt.float32
+BF16 = mybir.dt.bfloat16
+I32 = mybir.dt.int32
+U32 = mybir.dt.uint32
+U16 = mybir.dt.uint16
+U8 = mybir.dt.uint8
+FP8X4 = mybir.dt.float8_e4m3fn_x4
+FP4X4 = mybir.dt.float4_e2m1fn_x4
+ALU = mybir.AluOpType
+ACT = mybir.ActivationFunctionType
+
+P = 128
+PACK = 4
+KP = P * PACK
+NP = K // KP
+QN = 128
+
+
+def tile_list_flavour_pairing_appeal_kernel(
+    tc, tab_words, tab_scales, offs, offs2, w1_words, w1_scales, w2, w3_words, w3_scales, gain, zest, out
+):
+    nc = tc.nc
+    with ExitStack() as ctx:
+        keep = ctx.enter_context(tc.tile_pool(name="keep", bufs=1))
+        ring = ctx.enter_context(tc.tile_pool(name="ring", bufs=3))
+        psum = ctx.enter_context(tc.psum_pool(name="psum", bufs=2))
+
+        def held(name, shape, dtype):
+            return keep.tile(shape, dtype, name=name, align_bytes=64)
+
+        idx = keep.tile([P, S // 16], U16, name="idx")
+        idx2 = keep.tile([P, S2 // 16], U16, name="idx2")
+        tab_s = held("tab_s", [P, T], U8)
+        w_s = held("w_s", [P, NP * K], U8)
+        v_s1 = held("v_s1", [P, S], U8)
+        nc.vector.memset(tab_s[:].bitcast(I32), 0)
+        nc.gpsimd.memset(w_s[:].bitcast(I32), 0)
+        nc.vector.memset(v_s1[:].bitcast(I32), 0)
+
+        nc.sync.dma_start(idx[:], offs)
+        for q in range(4):
+            nc.scalar.dma_start(
+                out=tab_s[32 * q : 32 * q + 8, :].bitcast(I32),
+                in_=tab_scales[:, 4 * q : 4 * q + 4, :].bitcast(I32),
+            )
+        def load_w_scales(queue, src, r0):
+            for q in range(4):
+                queue.dma_start(
+                    out=w_s[32 * q + r0 : 32 * q + r0 + 4, :].rearrange("p (a c) -> p a c", a=NP).bitcast(I32),
+                    in_=src[:, 4 * q : 4 * q + 4, :].rearrange("a r c -> r a c").bitcast(I32),
+                )
+
+        load_w_scales(nc.gpsimd, w1_scales, 0)
+        gain_t = held("gain_t", [P, NP, PACK], F32)
+
+        tab = [held("tab%d" % a, [P, T], I32) for a in range(NP)]
+        w1_raw = held("w1_raw", [P, NP, K // 2], I32)
+        w3_raw = [held("w3_raw%d" % b, [P, NP, KP], I32) for b in range(NP)]
+        w2_raw = [[held("w2_raw%d%d" % (a, b), [P, PACK, KP], F32) for b in range(NP)] for a in range(NP)]
+
+        def load_tab(a):
+            nc.sync.dma_start(out=tab[a][:], in_=tab_words[a].rearrange("p t i -> p (t i)").bitcast(I32))
+
+        def load_w2(a, b):
+            nc.sync.dma_start(
+                out=w2_raw[a][b][:],
+                in_=w2[KP * a : KP * (a + 1), KP * b : KP * (b + 1)].rearrange("(p j) c -> p j c", j=PACK),
+            )
+
+        def load_w3(b):
+            nc.sync.dma_start(
+                out=w3_raw[b][:],
+                in_=w3_words.rearrange("a p c i -> p a (c i)")[:, :, 4 * KP * b : 4 * KP * (b + 1)].bitcast(I32),
+            )
+
+        load_tab(0)
+        load_w2(0, 0)
+        load_tab(1)
+        load_w_scales(nc.scalar, w3_scales, 4)
+        load_w3(0)
+        nc.sync.dma_start(out=w1_raw[:], in_=w1_words.rearrange("a p c -> p a c").bitcast(I32))
+        nc.sync.dma_start(idx2[:], offs2)
+        nc.sync.dma_start(out=gain_t[:], in_=gain.rearrange("(b p t) -> p b t", b=NP, t=PACK))
+        load_w2(1, 0)
+        load_w3(1)
+        load_w2(0, 1)
+        load_w2(1, 1)
+        zest_t = held("zest_t", [P, S2 // P], F32)
+        with nc.allow_non_contiguous_dma(reason="one value of zest for each partition"):
+            nc.sync.dma_start(out=zest_t[:], in_=zest.rearrange("(u p) -> p u", p=P))
+
+        v_s = held("v_s", [P, S], U8)
+        nc.vector.tensor_copy(v_s[:], tab_s[:].indirect(idx[:]))
+        nc.gpsimd.dma_start(out=v_s1[0 : P - 4, :].bitcast(I32), in_=v_s[4:P, :].bitcast(I32))
+        v_plane = [v_s, v_s1]
+        v_w = [held("v_w%d" % a, [P, S], U32) for a in range(NP)]
+        for a in range(NP):
+            nc.vector.tensor_copy(v_w[a][:], tab[a][:].bitcast(U32).indirect(idx[:]))
+
+        w3_d = [held("w3_d%d" % b, [P, NP, KP], U32) for b in range(NP)]
+        w1_d = [held("w1_d%d" % b, [P, NP, KP], U16) for b in range(NP)]
+        ws_d = [held("ws_d%d" % b, [P, NP, KP], U8) for b in range(NP)]
+
+        def deal(dst, src):
+            nc.vector.tensor_copy(
+                out=dst.rearrange("p a (t m) -> p a m t", t=PACK),
+                in_=src.rearrange("p a (m t) -> p a m t", t=PACK),
+            )
+
+        def deal_weights(b):
+            cols = slice(KP * b, KP * (b + 1))
+            deal(ws_d[b][:], w_s[:].rearrange("p (a c) -> p a c", a=NP)[:, :, cols])
+            deal(w3_d[b][:], w3_raw[b][:].bitcast(U32))
+            deal(w1_d[b][:], w1_raw[:].bitcast(U16)[:, :, cols])
+
+        w2_w = [[held("w2_w%d%d" % (a, b), [P, KP], U32) for b in range(NP)] for a in range(NP)]
+        w2_s = [[held("w2_s%d%d" % (a, b), [P, KP], U8) for b in range(NP)] for a in range(NP)]
+        w2_bf = [[held("w2_bf%d%d" % (a, b), [P, PACK * KP], BF16) for b in range(NP)] for a in range(NP)]
+
+        def cast_w2(a, b):
+            nc.scalar.copy(
+                out=w2_bf[a][b][:].rearrange("p (t m j) -> p m j t", t=PACK, j=PACK),
+                in_=w2_raw[a][b][:].rearrange("p j (m t) -> p m j t", t=PACK),
+            )
+
+        def quant_w2(a, b):
+            nc.vector.quantize_mx(out=w2_w[a][b][:].bitcast(FP8X4), scales=w2_s[a][b][:], in_=w2_bf[a][b][:])
+
+        v2_s = held("v2_s", [P, S2], U8)
+        v2_w = [held("v2_w%d" % a, [P, S2], U32) for a in range(NP)]
+        top = [held("top%d" % b, [P, PACK, S], F32) for b in range(NP)]
+        h_bf = [held("h_bf%d" % b, [P, S * PACK], BF16) for b in range(NP)]
+        h_w = [held("h_w%d" % b, [P, S], U32) for b in range(NP)]
+        h_s = [held("h_s%d" % b, [P, S], U8) for b in range(NP)]
+
+        def upper(b, t):
+            cols = slice(P * t, P * (t + 1))
+            raw = psum.tile([P, S], F32, name="raw")
+            for a in range(NP):
+                nc.tensor.matmul_mx(
+                    out=raw[:],
+                    lhsT=w3_d[b][:, a, cols].bitcast(FP8X4),
+                    lhsT_scale=ws_d[b][4:P, a, cols],
+                    rhs=v_w[a][:].bitcast(FP8X4),
+                    rhs_scale=v_plane[a][:],
+                    start=(a == 0),
+                    stop=(a == NP - 1),
+                )
+            blend = psum.tile([P, S], F32, name="blend")
+            for a in range(NP):
+                nc.tensor.matmul_mx(
+                    out=blend[:],
+                    lhsT=w1_d[b][:, a, cols].bitcast(FP4X4),
+                    lhsT_scale=ws_d[b][:, a, cols],
+                    rhs=v_w[a][:].bitcast(FP8X4),
+                    rhs_scale=v_plane[a][:],
+                    start=(a == 0),
+                    stop=(a == NP - 1),
+                )
+            gained = ring.tile([P, S], F32, name="gained")
+            nc.scalar.activation(gained[:], raw[:], ACT.Copy, scale=gain_t[:, b, t : t + 1])
+            nc.vector.tensor_tensor(top[b][:, t, :], blend[:], gained[:], ALU.max)
+
+        def lower(b, q):
+            js = slice(QN * q, QN * (q + 1))
+            base = psum.tile([P, PACK, QN], F32, name="base")
+            for t in range(PACK):
+                cols = slice(P * t, P * (t + 1))
+                for a in range(NP):
+                    nc.tensor.matmul_mx(
+                        out=base[:, t, :],
+                        lhsT=w2_w[a][b][:, cols].bitcast(FP8X4),
+                        lhsT_scale=w2_s[a][b][:, cols],
+                        rhs=v_w[a][:, js].bitcast(FP8X4),
+                        rhs_scale=v_plane[a][:, js],
+                        start=(a == 0),
+                        stop=(a == NP - 1),
+                    )
+            nc.vector.tensor_tensor(
+                h_bf[b][:, PACK * QN * q : PACK * QN * (q + 1)].rearrange("p (c i t) -> p c t i", i=2, t=PACK),
+                base[:].rearrange("p t (c i) -> p c t i", i=2),
+                top[b][:, :, js].rearrange("p t (c i) -> p c t i", i=2),
+                ALU.subtract,
+            )
+
+        cast_w2(0, 0)
+        deal_weights(0)
+        quant_w2(0, 0)
+        cast_w2(1, 0)
+        for t in range(PACK):
+            upper(0, t)
+        quant_w2(1, 0)
+        deal_weights(1)
+        cast_w2(0, 1)
+        for q in range(S // QN):
+            lower(0, q)
+        for t in range(PACK):
+            upper(1, t)
+        nc.vector.quantize_mx(out=h_w[0][:].bitcast(FP8X4), scales=h_s[0][:], in_=h_bf[0][:])
+        cast_w2(1, 1)
+        quant_w2(0, 1)
+        quant_w2(1, 1)
+        for q in range(S // QN):
+            lower(1, q)
+        nc.vector.quantize_mx(out=h_w[1][:].bitcast(FP8X4), scales=h_s[1][:], in_=h_bf[1][:])
+
+        nc.vector.tensor_copy(v2_s[:], tab_s[:].indirect(idx2[:]))
+        for a in range(NP):
+            nc.vector.tensor_copy(v2_w[a][:], tab[a][:].bitcast(U32).indirect(idx2[:]))
+
+        for u in range(S2 // P):
+            cols = slice(P * u, P * (u + 1))
+            match = psum.tile([P, S], F32, name="match")
+            for b in range(NP):
+                nc.tensor.matmul_mx(
+                    out=match[:],
+                    lhsT=v2_w[b][:, cols].bitcast(FP8X4),
+                    lhsT_scale=v2_s[4 * b : P, cols],
+                    rhs=h_w[b][:].bitcast(FP8X4),
+                    rhs_scale=h_s[b][:],
+                    start=(b == 0),
+                    stop=(b == NP - 1),
+                )
+            wave = ring.tile([P, S], F32, name="wave")
+            nc.scalar.activation(wave[:], match[:], ACT.Sin)
+            res = ring.tile([P, S], F32, name="res")
+            nc.vector.scalar_tensor_tensor(res[:], wave[:], zest_t[:, u : u + 1], match[:], ALU.mult, ALU.add)
+            nc.sync.dma_start(out=out[cols, :], in_=res[:])

@@ -30,7 +30,7 @@ def tile_list_flavour_pairing_appeal_kernel(
     with ExitStack() as ctx:
         keep = ctx.enter_context(tc.tile_pool(name="keep", bufs=1))
         ring = ctx.enter_context(tc.tile_pool(name="ring", bufs=3))
-        psum = ctx.enter_context(tc.psum_pool(name="psum", bufs=2))
+        psum = ctx.enter_context(tc.psum_pool(name="psum", bufs=8))
 
         def held(name, shape, dtype):
             return keep.tile(shape, dtype, name=name, align_bytes=64)
@@ -40,16 +40,13 @@ def tile_list_flavour_pairing_appeal_kernel(
         tab_s = held("tab_s", [P, T], U8)
         w_s = held("w_s", [P, NP * K], U8)
         v_s1 = held("v_s1", [P, S], U8)
-        nc.vector.memset(tab_s[:].bitcast(I32), 0)
-        nc.gpsimd.memset(w_s[:].bitcast(I32), 0)
+        nc.gpsimd.memset(tab_s[:].bitcast(I32), 0)
+        nc.vector.memset(w_s[:].bitcast(I32), 0)
         nc.vector.memset(v_s1[:].bitcast(I32), 0)
+        warm = held("warm", [P, 2], F32)
+        nc.vector.memset(warm[:], 0.0)
+        warm_out = held("warm_out", [P, 2], F32)
 
-        nc.sync.dma_start(idx[:], offs)
-        for q in range(4):
-            nc.scalar.dma_start(
-                out=tab_s[32 * q : 32 * q + 8, :].bitcast(I32),
-                in_=tab_scales[:, 4 * q : 4 * q + 4, :].bitcast(I32),
-            )
         def load_w_scales(queue, src, r0):
             for q in range(4):
                 queue.dma_start(
@@ -57,11 +54,10 @@ def tile_list_flavour_pairing_appeal_kernel(
                     in_=src[:, 4 * q : 4 * q + 4, :].rearrange("a r c -> r a c").bitcast(I32),
                 )
 
-        load_w_scales(nc.gpsimd, w1_scales, 0)
         gain_t = held("gain_t", [P, NP, PACK], F32)
 
         tab = [held("tab%d" % a, [P, T], I32) for a in range(NP)]
-        w1_raw = held("w1_raw", [P, NP, K // 2], I32)
+        w1_raw = [held("w1_raw%d" % b, [P, NP, KP // 2], I32) for b in range(NP)]
         w3_raw = [held("w3_raw%d" % b, [P, NP, KP], I32) for b in range(NP)]
         w2_raw = [[held("w2_raw%d%d" % (a, b), [P, PACK, KP], F32) for b in range(NP)] for a in range(NP)]
 
@@ -80,16 +76,31 @@ def tile_list_flavour_pairing_appeal_kernel(
                 in_=w3_words.rearrange("a p c i -> p a (c i)")[:, :, 4 * KP * b : 4 * KP * (b + 1)].bitcast(I32),
             )
 
+        def load_w1(b):
+            nc.sync.dma_start(
+                out=w1_raw[b][:],
+                in_=w1_words.rearrange("a p c -> p a c")[:, :, 2 * KP * b : 2 * KP * (b + 1)].bitcast(I32),
+            )
+
+        nc.sync.dma_start(idx[:], offs)
+        for q in range(4):
+            nc.scalar.dma_start(
+                out=tab_s[32 * q : 32 * q + 8, :].bitcast(I32),
+                in_=tab_scales[:, 4 * q : 4 * q + 4, :].bitcast(I32),
+            )
         load_tab(0)
-        load_w2(0, 0)
         load_tab(1)
-        load_w_scales(nc.scalar, w3_scales, 4)
-        load_w3(0)
-        nc.sync.dma_start(out=w1_raw[:], in_=w1_words.rearrange("a p c -> p a c").bitcast(I32))
         nc.sync.dma_start(idx2[:], offs2)
+        load_w_scales(nc.scalar, w3_scales, 4)
+        load_w_scales(nc.scalar, w1_scales, 0)
+        nc.scalar.activation(warm_out[:], warm[:], ACT.Sin)
+        load_w3(0)
+        load_w1(0)
+        load_w2(0, 0)
         nc.sync.dma_start(out=gain_t[:], in_=gain.rearrange("(b p t) -> p b t", b=NP, t=PACK))
-        load_w2(1, 0)
         load_w3(1)
+        load_w1(1)
+        load_w2(1, 0)
         load_w2(0, 1)
         load_w2(1, 1)
         zest_t = held("zest_t", [P, S2 // P], F32)
@@ -98,7 +109,7 @@ def tile_list_flavour_pairing_appeal_kernel(
 
         v_s = held("v_s", [P, S], U8)
         nc.vector.tensor_copy(v_s[:], tab_s[:].indirect(idx[:]))
-        nc.gpsimd.dma_start(out=v_s1[0 : P - 4, :].bitcast(I32), in_=v_s[4:P, :].bitcast(I32))
+        nc.scalar.dma_start(out=v_s1[0:100, :].bitcast(I32), in_=v_s[4:104, :].bitcast(I32))
         v_plane = [v_s, v_s1]
         v_w = [held("v_w%d" % a, [P, S], U32) for a in range(NP)]
         for a in range(NP):
@@ -118,23 +129,22 @@ def tile_list_flavour_pairing_appeal_kernel(
             cols = slice(KP * b, KP * (b + 1))
             deal(ws_d[b][:], w_s[:].rearrange("p (a c) -> p a c", a=NP)[:, :, cols])
             deal(w3_d[b][:], w3_raw[b][:].bitcast(U32))
-            deal(w1_d[b][:], w1_raw[:].bitcast(U16)[:, :, cols])
+            deal(w1_d[b][:], w1_raw[b][:].bitcast(U16))
 
         w2_w = [[held("w2_w%d%d" % (a, b), [P, KP], U32) for b in range(NP)] for a in range(NP)]
         w2_s = [[held("w2_s%d%d" % (a, b), [P, KP], U8) for b in range(NP)] for a in range(NP)]
         w2_bf = [[held("w2_bf%d%d" % (a, b), [P, PACK * KP], BF16) for b in range(NP)] for a in range(NP)]
 
-        def cast_w2(a, b):
+        def cast_w2(a, b, part):
+            ms = slice(32 * part, 32 * (part + 1))
             nc.scalar.copy(
-                out=w2_bf[a][b][:].rearrange("p (t m j) -> p m j t", t=PACK, j=PACK),
-                in_=w2_raw[a][b][:].rearrange("p j (m t) -> p m j t", t=PACK),
+                out=w2_bf[a][b][:].rearrange("p (t m j) -> p m j t", t=PACK, j=PACK)[:, ms],
+                in_=w2_raw[a][b][:].rearrange("p j (m t) -> p m j t", t=PACK)[:, ms],
             )
 
         def quant_w2(a, b):
             nc.vector.quantize_mx(out=w2_w[a][b][:].bitcast(FP8X4), scales=w2_s[a][b][:], in_=w2_bf[a][b][:])
 
-        v2_s = held("v2_s", [P, S2], U8)
-        v2_w = [held("v2_w%d" % a, [P, S2], U32) for a in range(NP)]
         top = [held("top%d" % b, [P, PACK, S], F32) for b in range(NP)]
         h_bf = [held("h_bf%d" % b, [P, S * PACK], BF16) for b in range(NP)]
         h_w = [held("h_w%d" % b, [P, S], U32) for b in range(NP)]
@@ -142,7 +152,7 @@ def tile_list_flavour_pairing_appeal_kernel(
 
         def upper(b, t):
             cols = slice(P * t, P * (t + 1))
-            raw = psum.tile([P, S], F32, name="raw")
+            raw = psum.tile([P, S], F32, name="bank")
             for a in range(NP):
                 nc.tensor.matmul_mx(
                     out=raw[:],
@@ -153,7 +163,7 @@ def tile_list_flavour_pairing_appeal_kernel(
                     start=(a == 0),
                     stop=(a == NP - 1),
                 )
-            blend = psum.tile([P, S], F32, name="blend")
+            blend = psum.tile([P, S], F32, name="bank")
             for a in range(NP):
                 nc.tensor.matmul_mx(
                     out=blend[:],
@@ -164,13 +174,13 @@ def tile_list_flavour_pairing_appeal_kernel(
                     start=(a == 0),
                     stop=(a == NP - 1),
                 )
-            gained = ring.tile([P, S], F32, name="gained")
+            gained = held("gained%d%d" % (b, t), [P, S], F32)
             nc.scalar.activation(gained[:], raw[:], ACT.Copy, scale=gain_t[:, b, t : t + 1])
             nc.vector.tensor_tensor(top[b][:, t, :], blend[:], gained[:], ALU.max)
 
         def lower(b, q):
             js = slice(QN * q, QN * (q + 1))
-            base = psum.tile([P, PACK, QN], F32, name="base")
+            base = psum.tile([P, PACK, QN], F32, name="bank")
             for t in range(PACK):
                 cols = slice(P * t, P * (t + 1))
                 for a in range(NP):
@@ -190,39 +200,43 @@ def tile_list_flavour_pairing_appeal_kernel(
                 ALU.subtract,
             )
 
-        cast_w2(0, 0)
-        deal_weights(0)
-        quant_w2(0, 0)
-        cast_w2(1, 0)
-        for t in range(PACK):
-            upper(0, t)
-        quant_w2(1, 0)
-        deal_weights(1)
-        cast_w2(0, 1)
-        for q in range(S // QN):
-            lower(0, q)
-        for t in range(PACK):
-            upper(1, t)
-        nc.vector.quantize_mx(out=h_w[0][:].bitcast(FP8X4), scales=h_s[0][:], in_=h_bf[0][:])
-        cast_w2(1, 1)
-        quant_w2(0, 1)
-        quant_w2(1, 1)
-        for q in range(S // QN):
-            lower(1, q)
-        nc.vector.quantize_mx(out=h_w[1][:].bitcast(FP8X4), scales=h_s[1][:], in_=h_bf[1][:])
+        def gather_menu(dst, window, half):
+            nc.vector.tensor_copy(dst, window.indirect(idx2[:, S // 16 * half : S // 16 * (half + 1)]))
 
-        nc.vector.tensor_copy(v2_s[:], tab_s[:].indirect(idx2[:]))
-        for a in range(NP):
-            nc.vector.tensor_copy(v2_w[a][:], tab[a][:].bitcast(U32).indirect(idx2[:]))
+        deal_weights(0)
+        deal_weights(1)
+        for b in range(NP):
+            for t in range(PACK):
+                upper(b, t)
+        for b in range(NP):
+            for a in range(NP):
+                for part in range(4):
+                    cast_w2(a, b, part)
+                quant_w2(a, b)
+        for b in range(NP):
+            for q in range(S // QN):
+                lower(b, q)
+            nc.vector.quantize_mx(out=h_w[b][:].bitcast(FP8X4), scales=h_s[b][:], in_=h_bf[b][:])
+        v2_s = [held("v2_s0", [P, S], U8), held("v2_s1", [P, S], U8)]
+        late = keep.tile([P, NP * S], U32, name="late", tag="h_bf1", align_bytes=64)
+        v2_w = [
+            [held("v2_w0%d" % a, [P, S], U32)[:] for a in range(NP)],
+            [late[:, S * a : S * (a + 1)] for a in range(NP)],
+        ]
+        for half in range(2):
+            gather_menu(v2_s[half][:], tab_s[:], half)
+            for a in range(NP):
+                gather_menu(v2_w[half][a], tab[a][:].bitcast(U32), half)
 
         for u in range(S2 // P):
             cols = slice(P * u, P * (u + 1))
-            match = psum.tile([P, S], F32, name="match")
+            half, mc = u // 4, slice(P * (u % 4), P * (u % 4 + 1))
+            match = psum.tile([P, S], F32, name="bank")
             for b in range(NP):
                 nc.tensor.matmul_mx(
                     out=match[:],
-                    lhsT=v2_w[b][:, cols].bitcast(FP8X4),
-                    lhsT_scale=v2_s[4 * b : P, cols],
+                    lhsT=v2_w[half][b][:, mc].bitcast(FP8X4),
+                    lhsT_scale=v2_s[half][4 * b : P, mc],
                     rhs=h_w[b][:].bitcast(FP8X4),
                     rhs_scale=h_s[b][:],
                     start=(b == 0),
@@ -230,6 +244,6 @@ def tile_list_flavour_pairing_appeal_kernel(
                 )
             wave = ring.tile([P, S], F32, name="wave")
             nc.scalar.activation(wave[:], match[:], ACT.Sin)
-            res = ring.tile([P, S], F32, name="res")
+            res = held("res%d" % u, [P, S], F32)
             nc.vector.scalar_tensor_tensor(res[:], wave[:], zest_t[:, u : u + 1], match[:], ALU.mult, ALU.add)
             nc.sync.dma_start(out=out[cols, :], in_=res[:])

@@ -1,6 +1,7 @@
 from contextlib import ExitStack
 
 import concourse.mybir as mybir
+from concourse.masks import make_identity
 
 K, T, S, S2 = 1024, 2048, 512, 1024
 FLOPS = 2 * K * K * S * 3 + 2 * K * S2 * S
@@ -46,15 +47,19 @@ def tile_list_flavour_pairing_appeal_kernel(
         warm = held("warm", [P, 2], F32)
         nc.vector.memset(warm[:], 0.0)
         warm_out = held("warm_out", [P, 2], F32)
+        nc.scalar.activation(warm_out[:], warm[:], ACT.Sin)
 
-        def load_w_scales(queue, src, r0):
-            for q in range(4):
+        def load_w_scales(queue, src, r0, quadrants):
+            for q in quadrants:
                 queue.dma_start(
                     out=w_s[32 * q + r0 : 32 * q + r0 + 4, :].rearrange("p (a c) -> p a c", a=NP).bitcast(I32),
                     in_=src[:, 4 * q : 4 * q + 4, :].rearrange("a r c -> r a c").bitcast(I32),
                 )
 
-        gain_t = held("gain_t", [P, NP, PACK], F32)
+        rows = held("rows", [P, KP + P], F32)
+        nc.vector.memset(rows[:], 0.0)
+        ident = held("ident", [P, P], F32)
+        make_identity(nc, ident[:])
 
         tab = [held("tab%d" % a, [P, T], I32) for a in range(NP)]
         w1_raw = [held("w1_raw%d" % b, [P, NP, KP // 2], I32) for b in range(NP)]
@@ -82,30 +87,36 @@ def tile_list_flavour_pairing_appeal_kernel(
                 in_=w1_words.rearrange("a p c -> p a c")[:, :, 2 * KP * b : 2 * KP * (b + 1)].bitcast(I32),
             )
 
+        load_w_scales(nc.gpsimd, w1_scales, 0, range(4))
         nc.sync.dma_start(idx[:], offs)
+        load_tab(0)
         for q in range(4):
-            nc.scalar.dma_start(
+            nc.sync.dma_start(
                 out=tab_s[32 * q : 32 * q + 8, :].bitcast(I32),
                 in_=tab_scales[:, 4 * q : 4 * q + 4, :].bitcast(I32),
             )
-        load_tab(0)
-        load_tab(1)
-        nc.sync.dma_start(idx2[:], offs2)
-        load_w_scales(nc.scalar, w3_scales, 4)
-        load_w_scales(nc.scalar, w1_scales, 0)
-        nc.scalar.activation(warm_out[:], warm[:], ACT.Sin)
-        load_w3(0)
         load_w1(0)
+        nc.sync.dma_start(idx2[:], offs2)
+        load_w3(0)
+        load_tab(1)
+        load_w_scales(nc.sync, w3_scales, 4, range(4))
         load_w2(0, 0)
-        nc.sync.dma_start(out=gain_t[:], in_=gain.rearrange("(b p t) -> p b t", b=NP, t=PACK))
+        nc.sync.dma_start(out=rows[0:NP, 0:KP], in_=gain.rearrange("(b c) -> b c", b=NP))
+        nc.sync.dma_start(out=rows[0 : S2 // P, KP:], in_=zest.rearrange("(u p) -> u p", p=P))
+        load_w2(1, 0)
         load_w3(1)
         load_w1(1)
-        load_w2(1, 0)
         load_w2(0, 1)
         load_w2(1, 1)
+        gain_t = held("gain_t", [P, PACK, NP], F32)
+        turned = psum.tile([P, PACK, P], F32, name="bank")
+        for t in range(PACK):
+            nc.tensor.transpose(turned[:, t, :], rows[:, t:KP:PACK], ident[:])
+        nc.scalar.copy(out=gain_t[:], in_=turned[:, :, 0:NP])
         zest_t = held("zest_t", [P, S2 // P], F32)
-        with nc.allow_non_contiguous_dma(reason="one value of zest for each partition"):
-            nc.sync.dma_start(out=zest_t[:], in_=zest.rearrange("(u p) -> p u", p=P))
+        turned = psum.tile([P, P], F32, name="bank")
+        nc.tensor.transpose(turned[:], rows[:, KP:], ident[:])
+        nc.scalar.copy(out=zest_t[:], in_=turned[:, 0 : S2 // P])
 
         v_s = held("v_s", [P, S], U8)
         nc.vector.tensor_copy(v_s[:], tab_s[:].indirect(idx[:]))
@@ -121,14 +132,17 @@ def tile_list_flavour_pairing_appeal_kernel(
 
         def deal(dst, src):
             nc.vector.tensor_copy(
-                out=dst.rearrange("p a (t m) -> p a m t", t=PACK),
-                in_=src.rearrange("p a (m t) -> p a m t", t=PACK),
+                out=dst.rearrange("p a (t m) -> p a t m", t=PACK),
+                in_=src.rearrange("p a (m t) -> p a t m", t=PACK),
             )
 
         def deal_weights(b):
             cols = slice(KP * b, KP * (b + 1))
             deal(ws_d[b][:], w_s[:].rearrange("p (a c) -> p a c", a=NP)[:, :, cols])
-            deal(w3_d[b][:], w3_raw[b][:].bitcast(U32))
+            nc.vector.tensor_copy(
+                out=w3_d[b][:].rearrange("p a (t c i) -> p a c t i", t=PACK, i=2),
+                in_=w3_raw[b][:].bitcast(U32).rearrange("p a (c i t) -> p a c t i", t=PACK, i=2),
+            )
             deal(w1_d[b][:], w1_raw[b][:].bitcast(U16))
 
         w2_w = [[held("w2_w%d%d" % (a, b), [P, KP], U32) for b in range(NP)] for a in range(NP)]
@@ -136,10 +150,10 @@ def tile_list_flavour_pairing_appeal_kernel(
         w2_bf = [[held("w2_bf%d%d" % (a, b), [P, PACK * KP], BF16) for b in range(NP)] for a in range(NP)]
 
         def cast_w2(a, b, part):
-            ms = slice(32 * part, 32 * (part + 1))
+            ms = slice(64 * part, 64 * (part + 1))
             nc.scalar.copy(
-                out=w2_bf[a][b][:].rearrange("p (t m j) -> p m j t", t=PACK, j=PACK)[:, ms],
-                in_=w2_raw[a][b][:].rearrange("p j (m t) -> p m j t", t=PACK)[:, ms],
+                out=w2_bf[a][b][:].rearrange("p (u i m j) -> p m u j i", u=2, i=2, j=PACK)[:, ms],
+                in_=w2_raw[a][b][:].rearrange("p j (m u i) -> p m u j i", u=2, i=2)[:, ms],
             )
 
         def quant_w2(a, b):
@@ -175,7 +189,7 @@ def tile_list_flavour_pairing_appeal_kernel(
                     stop=(a == NP - 1),
                 )
             gained = held("gained%d%d" % (b, t), [P, S], F32)
-            nc.scalar.activation(gained[:], raw[:], ACT.Copy, scale=gain_t[:, b, t : t + 1])
+            nc.scalar.activation(gained[:], raw[:], ACT.Copy, scale=gain_t[:, t, b : b + 1])
             nc.vector.tensor_tensor(top[b][:, t, :], blend[:], gained[:], ALU.max)
 
         def lower(b, q):
@@ -208,25 +222,31 @@ def tile_list_flavour_pairing_appeal_kernel(
         for b in range(NP):
             for t in range(PACK):
                 upper(b, t)
-        for b in range(NP):
             for a in range(NP):
-                for part in range(4):
+                for part in range(2):
                     cast_w2(a, b, part)
                 quant_w2(a, b)
-        for b in range(NP):
             for q in range(S // QN):
                 lower(b, q)
-            nc.vector.quantize_mx(out=h_w[b][:].bitcast(FP8X4), scales=h_s[b][:], in_=h_bf[b][:])
-        v2_s = [held("v2_s0", [P, S], U8), held("v2_s1", [P, S], U8)]
-        late = keep.tile([P, NP * S], U32, name="late", tag="h_bf1", align_bytes=64)
+                if q % 2 == 1:
+                    js = slice(QN * (q - 1), QN * (q + 1))
+                    nc.vector.quantize_mx(
+                        out=h_w[b][:, js].bitcast(FP8X4),
+                        scales=h_s[b][:, js],
+                        in_=h_bf[b][:, PACK * js.start : PACK * js.stop],
+                    )
+        def reuse(name, tag, dtype):
+            return keep.tile([P, S], dtype, name=name, tag=tag, align_bytes=64)
+
+        v2_s = [reuse("v2_s0", "v2_s0", U8), reuse("v2_s1", "w_s", U8)]
         v2_w = [
-            [held("v2_w0%d" % a, [P, S], U32)[:] for a in range(NP)],
-            [late[:, S * a : S * (a + 1)] for a in range(NP)],
+            [reuse("v2_w00", "v2_w00", U32), reuse("v2_w01", "w3_raw0", U32)],
+            [reuse("v2_w10", "gained00", U32), reuse("v2_w11", "h_bf1", U32)],
         ]
         for half in range(2):
             gather_menu(v2_s[half][:], tab_s[:], half)
             for a in range(NP):
-                gather_menu(v2_w[half][a], tab[a][:].bitcast(U32), half)
+                gather_menu(v2_w[half][a][:], tab[a][:].bitcast(U32), half)
 
         for u in range(S2 // P):
             cols = slice(P * u, P * (u + 1))
@@ -245,5 +265,10 @@ def tile_list_flavour_pairing_appeal_kernel(
             wave = ring.tile([P, S], F32, name="wave")
             nc.scalar.activation(wave[:], match[:], ACT.Sin)
             res = held("res%d" % u, [P, S], F32)
-            nc.vector.scalar_tensor_tensor(res[:], wave[:], zest_t[:, u : u + 1], match[:], ALU.mult, ALU.add)
-            nc.sync.dma_start(out=out[cols, :], in_=res[:])
+            pieces = 2 if u == S2 // P - 1 else 1
+            for piece in range(pieces):
+                js = slice(S // pieces * piece, S // pieces * (piece + 1))
+                nc.vector.scalar_tensor_tensor(
+                    res[:, js], wave[:, js], zest_t[:, u : u + 1], match[:, js], ALU.mult, ALU.add
+                )
+                nc.sync.dma_start(out=out[cols, js], in_=res[:, js])

from contextlib import ExitStack

import concourse.mybir as mybir
from concourse.masks import make_identity

K, T, S, S2 = 1024, 2048, 512, 1024
FLOPS = 2 * K * K * S * 3 + 2 * K * S2 * S

F32 = mybir.dt.float32
BF16 = mybir.dt.bfloat16
I32 = mybir.dt.int32
U32 = mybir.dt.uint32
U16 = mybir.dt.uint16
U8 = mybir.dt.uint8
FP8X4 = mybir.dt.float8_e4m3fn_x4
FP4X4 = mybir.dt.float4_e2m1fn_x4
ALU = mybir.AluOpType
ACT = mybir.ActivationFunctionType

P = 128
PACK = 4
KP = P * PACK
NP = K // KP
QN = 128


def tile_list_flavour_pairing_appeal_kernel(
    tc, tab_words, tab_scales, offs, offs2, w1_words, w1_scales, w2, w3_words, w3_scales, gain, zest, out
):
    nc = tc.nc
    with ExitStack() as ctx:
        keep = ctx.enter_context(tc.tile_pool(name="keep", bufs=1))
        ring = ctx.enter_context(tc.tile_pool(name="ring", bufs=3))
        psum = ctx.enter_context(tc.psum_pool(name="psum", bufs=8))

        def held(name, shape, dtype):
            return keep.tile(shape, dtype, name=name, align_bytes=64)

        idx = keep.tile([P, S // 16], U16, name="idx")
        idx2 = keep.tile([P, S2 // 16], U16, name="idx2")
        tab_s = held("tab_s", [P, T], U8)
        w_s = held("w_s", [P, NP * K], U8)
        v_s1 = held("v_s1", [P, S], U8)
        nc.gpsimd.memset(tab_s[:].bitcast(I32), 0)
        nc.vector.memset(w_s[:].bitcast(I32), 0)
        nc.vector.memset(v_s1[:].bitcast(I32), 0)
        warm = held("warm", [P, 2], F32)
        nc.vector.memset(warm[:], 0.0)
        warm_out = held("warm_out", [P, 2], F32)
        nc.scalar.activation(warm_out[:], warm[:], ACT.Sin)

        def load_w_scales(queue, src, r0, quadrants):
            for q in quadrants:
                queue.dma_start(
                    out=w_s[32 * q + r0 : 32 * q + r0 + 4, :].rearrange("p (a c) -> p a c", a=NP).bitcast(I32),
                    in_=src[:, 4 * q : 4 * q + 4, :].rearrange("a r c -> r a c").bitcast(I32),
                )

        rows = held("rows", [P, KP + P], F32)
        nc.vector.memset(rows[:], 0.0)
        ident = held("ident", [P, P], F32)
        make_identity(nc, ident[:])

        tab = [held("tab%d" % a, [P, T], I32) for a in range(NP)]
        w1_raw = [held("w1_raw%d" % b, [P, NP, KP // 2], I32) for b in range(NP)]
        w3_raw = [held("w3_raw%d" % b, [P, NP, KP], I32) for b in range(NP)]
        w2_raw = [[held("w2_raw%d%d" % (a, b), [P, PACK, KP], F32) for b in range(NP)] for a in range(NP)]

        def load_tab(a):
            nc.sync.dma_start(out=tab[a][:], in_=tab_words[a].rearrange("p t i -> p (t i)").bitcast(I32))

        def load_w2(a, b):
            nc.sync.dma_start(
                out=w2_raw[a][b][:],
                in_=w2[KP * a : KP * (a + 1), KP * b : KP * (b + 1)].rearrange("(p j) c -> p j c", j=PACK),
            )

        def load_w3(b):
            nc.sync.dma_start(
                out=w3_raw[b][:],
                in_=w3_words.rearrange("a p c i -> p a (c i)")[:, :, 4 * KP * b : 4 * KP * (b + 1)].bitcast(I32),
            )

        def load_w1(b):
            nc.sync.dma_start(
                out=w1_raw[b][:],
                in_=w1_words.rearrange("a p c -> p a c")[:, :, 2 * KP * b : 2 * KP * (b + 1)].bitcast(I32),
            )

        load_w_scales(nc.gpsimd, w1_scales, 0, range(4))
        nc.sync.dma_start(idx[:], offs)
        load_tab(0)
        for q in range(4):
            nc.sync.dma_start(
                out=tab_s[32 * q : 32 * q + 8, :].bitcast(I32),
                in_=tab_scales[:, 4 * q : 4 * q + 4, :].bitcast(I32),
            )
        load_w1(0)
        nc.sync.dma_start(idx2[:], offs2)
        load_w3(0)
        load_tab(1)
        load_w_scales(nc.sync, w3_scales, 4, range(4))
        load_w2(0, 0)
        nc.sync.dma_start(out=rows[0:NP, 0:KP], in_=gain.rearrange("(b c) -> b c", b=NP))
        nc.sync.dma_start(out=rows[0 : S2 // P, KP:], in_=zest.rearrange("(u p) -> u p", p=P))
        load_w2(1, 0)
        load_w3(1)
        load_w1(1)
        load_w2(0, 1)
        load_w2(1, 1)
        gain_t = held("gain_t", [P, PACK, NP], F32)
        turned = psum.tile([P, PACK, P], F32, name="bank")
        for t in range(PACK):
            nc.tensor.transpose(turned[:, t, :], rows[:, t:KP:PACK], ident[:])
        nc.scalar.copy(out=gain_t[:], in_=turned[:, :, 0:NP])
        zest_t = held("zest_t", [P, S2 // P], F32)
        turned = psum.tile([P, P], F32, name="bank")
        nc.tensor.transpose(turned[:], rows[:, KP:], ident[:])
        nc.scalar.copy(out=zest_t[:], in_=turned[:, 0 : S2 // P])

        v_s = held("v_s", [P, S], U8)
        nc.vector.tensor_copy(v_s[:], tab_s[:].indirect(idx[:]))
        nc.scalar.dma_start(out=v_s1[0:100, :].bitcast(I32), in_=v_s[4:104, :].bitcast(I32))
        v_plane = [v_s, v_s1]
        v_w = [held("v_w%d" % a, [P, S], U32) for a in range(NP)]
        for a in range(NP):
            nc.vector.tensor_copy(v_w[a][:], tab[a][:].bitcast(U32).indirect(idx[:]))

        w3_d = [held("w3_d%d" % b, [P, NP, KP], U32) for b in range(NP)]
        w1_d = [held("w1_d%d" % b, [P, NP, KP], U16) for b in range(NP)]
        ws_d = [held("ws_d%d" % b, [P, NP, KP], U8) for b in range(NP)]

        def deal(dst, src):
            nc.vector.tensor_copy(
                out=dst.rearrange("p a (t m) -> p a t m", t=PACK),
                in_=src.rearrange("p a (m t) -> p a t m", t=PACK),
            )

        def deal_weights(b):
            cols = slice(KP * b, KP * (b + 1))
            deal(ws_d[b][:], w_s[:].rearrange("p (a c) -> p a c", a=NP)[:, :, cols])
            nc.vector.tensor_copy(
                out=w3_d[b][:].rearrange("p a (t c i) -> p a c t i", t=PACK, i=2),
                in_=w3_raw[b][:].bitcast(U32).rearrange("p a (c i t) -> p a c t i", t=PACK, i=2),
            )
            deal(w1_d[b][:], w1_raw[b][:].bitcast(U16))

        w2_w = [[held("w2_w%d%d" % (a, b), [P, KP], U32) for b in range(NP)] for a in range(NP)]
        w2_s = [[held("w2_s%d%d" % (a, b), [P, KP], U8) for b in range(NP)] for a in range(NP)]
        w2_bf = [[held("w2_bf%d%d" % (a, b), [P, PACK * KP], BF16) for b in range(NP)] for a in range(NP)]

        def cast_w2(a, b, part):
            ms = slice(64 * part, 64 * (part + 1))
            nc.scalar.copy(
                out=w2_bf[a][b][:].rearrange("p (u i m j) -> p m u j i", u=2, i=2, j=PACK)[:, ms],
                in_=w2_raw[a][b][:].rearrange("p j (m u i) -> p m u j i", u=2, i=2)[:, ms],
            )

        def quant_w2(a, b):
            nc.vector.quantize_mx(out=w2_w[a][b][:].bitcast(FP8X4), scales=w2_s[a][b][:], in_=w2_bf[a][b][:])

        top = [held("top%d" % b, [P, PACK, S], F32) for b in range(NP)]
        h_bf = [held("h_bf%d" % b, [P, S * PACK], BF16) for b in range(NP)]
        h_w = [held("h_w%d" % b, [P, S], U32) for b in range(NP)]
        h_s = [held("h_s%d" % b, [P, S], U8) for b in range(NP)]

        def upper(b, t):
            cols = slice(P * t, P * (t + 1))
            raw = psum.tile([P, S], F32, name="bank")
            for a in range(NP):
                nc.tensor.matmul_mx(
                    out=raw[:],
                    lhsT=w3_d[b][:, a, cols].bitcast(FP8X4),
                    lhsT_scale=ws_d[b][4:P, a, cols],
                    rhs=v_w[a][:].bitcast(FP8X4),
                    rhs_scale=v_plane[a][:],
                    start=(a == 0),
                    stop=(a == NP - 1),
                )
            blend = psum.tile([P, S], F32, name="bank")
            for a in range(NP):
                nc.tensor.matmul_mx(
                    out=blend[:],
                    lhsT=w1_d[b][:, a, cols].bitcast(FP4X4),
                    lhsT_scale=ws_d[b][:, a, cols],
                    rhs=v_w[a][:].bitcast(FP8X4),
                    rhs_scale=v_plane[a][:],
                    start=(a == 0),
                    stop=(a == NP - 1),
                )
            gained = held("gained%d%d" % (b, t), [P, S], F32)
            nc.scalar.activation(gained[:], raw[:], ACT.Copy, scale=gain_t[:, t, b : b + 1])
            nc.vector.tensor_tensor(top[b][:, t, :], blend[:], gained[:], ALU.max)

        def lower(b, q):
            js = slice(QN * q, QN * (q + 1))
            base = psum.tile([P, PACK, QN], F32, name="bank")
            for t in range(PACK):
                cols = slice(P * t, P * (t + 1))
                for a in range(NP):
                    nc.tensor.matmul_mx(
                        out=base[:, t, :],
                        lhsT=w2_w[a][b][:, cols].bitcast(FP8X4),
                        lhsT_scale=w2_s[a][b][:, cols],
                        rhs=v_w[a][:, js].bitcast(FP8X4),
                        rhs_scale=v_plane[a][:, js],
                        start=(a == 0),
                        stop=(a == NP - 1),
                    )
            nc.vector.tensor_tensor(
                h_bf[b][:, PACK * QN * q : PACK * QN * (q + 1)].rearrange("p (c i t) -> p c t i", i=2, t=PACK),
                base[:].rearrange("p t (c i) -> p c t i", i=2),
                top[b][:, :, js].rearrange("p t (c i) -> p c t i", i=2),
                ALU.subtract,
            )

        def gather_menu(dst, window, half):
            nc.vector.tensor_copy(dst, window.indirect(idx2[:, S // 16 * half : S // 16 * (half + 1)]))

        deal_weights(0)
        deal_weights(1)
        for b in range(NP):
            for t in range(PACK):
                upper(b, t)
            for a in range(NP):
                for part in range(2):
                    cast_w2(a, b, part)
                quant_w2(a, b)
            for q in range(S // QN):
                lower(b, q)
                if q % 2 == 1:
                    js = slice(QN * (q - 1), QN * (q + 1))
                    nc.vector.quantize_mx(
                        out=h_w[b][:, js].bitcast(FP8X4),
                        scales=h_s[b][:, js],
                        in_=h_bf[b][:, PACK * js.start : PACK * js.stop],
                    )
        def reuse(name, tag, dtype):
            return keep.tile([P, S], dtype, name=name, tag=tag, align_bytes=64)

        v2_s = [reuse("v2_s0", "v2_s0", U8), reuse("v2_s1", "w_s", U8)]
        v2_w = [
            [reuse("v2_w00", "v2_w00", U32), reuse("v2_w01", "w3_raw0", U32)],
            [reuse("v2_w10", "gained00", U32), reuse("v2_w11", "h_bf1", U32)],
        ]
        for half in range(2):
            gather_menu(v2_s[half][:], tab_s[:], half)
            for a in range(NP):
                gather_menu(v2_w[half][a][:], tab[a][:].bitcast(U32), half)

        for u in range(S2 // P):
            cols = slice(P * u, P * (u + 1))
            half, mc = u // 4, slice(P * (u % 4), P * (u % 4 + 1))
            match = psum.tile([P, S], F32, name="bank")
            for b in range(NP):
                nc.tensor.matmul_mx(
                    out=match[:],
                    lhsT=v2_w[half][b][:, mc].bitcast(FP8X4),
                    lhsT_scale=v2_s[half][4 * b : P, mc],
                    rhs=h_w[b][:].bitcast(FP8X4),
                    rhs_scale=h_s[b][:],
                    start=(b == 0),
                    stop=(b == NP - 1),
                )
            wave = ring.tile([P, S], F32, name="wave")
            nc.scalar.activation(wave[:], match[:], ACT.Sin)
            res = held("res%d" % u, [P, S], F32)
            pieces = 2 if u == S2 // P - 1 else 1
            for piece in range(pieces):
                js = slice(S // pieces * piece, S // pieces * (piece + 1))
                nc.vector.scalar_tensor_tensor(
                    res[:, js], wave[:, js], zest_t[:, u : u + 1], match[:, js], ALU.mult, ALU.add
                )
                nc.sync.dma_start(out=out[cols, js], in_=res[:, js])
